import numpy as np
import ml_dtypes


def mxq(x, axis, fmt="e4m3"):
    dtype, down = {"e4m3": (ml_dtypes.float8_e4m3fn, 7), "e5m2": (ml_dtypes.float8_e5m2, 14)}[fmt]
    v = np.moveaxis(np.asarray(x, np.float32).astype(ml_dtypes.bfloat16).astype(np.float64), axis, -1)
    blocks = v.reshape(v.shape[:-1] + (-1, 32))
    amax = np.abs(blocks).max(-1, keepdims=True)
    byte = np.maximum(np.where(amax > 0, np.frexp(amax)[1] - 1 + 127, 0) - down, 1)
    scale = np.exp2(byte - 127.0)
    codes = (blocks / scale).astype(np.float32).astype(dtype).astype(np.float64)
    return np.moveaxis((codes * scale).reshape(v.shape), -1, axis)


WIDE = False


def mx_kscale(k):
    if not WIDE:
        return np.ones(k)
    levels = np.array([10, -10, 5, -5, 0])
    if k % 512:
        return np.exp2(np.random.permutation(np.resize(levels, k // 32))).repeat(32)
    a = np.empty((k // 512, 16))
    for p in range(k // 512):
        a[p, :8] = np.random.permutation(np.resize(levels, 8))
        for g in range(8):
            far = levels[np.abs(levels - a[p, g]) >= 10]
            a[p, g + 8] = far[np.random.randint(len(far))]
    return np.exp2(a.ravel()).repeat(32)


def f64(x):
    return np.asarray(x).astype(np.float64)


def striped(idx):
    return np.tile(idx.reshape(-1, 16).T, (8, 1)).astype(np.uint16)


def unstriped(offs):
    return offs[:16].T.reshape(-1).astype(np.int64)


def pack_weight(w):
    k, n = w.shape
    w = f64(np.asarray(w, np.float32).astype(ml_dtypes.bfloat16)).reshape(k // 32, 32, n)
    amax = np.abs(w).max(1)
    byte = np.clip(np.where(amax > 0, np.frexp(amax)[1] - 1 + 127 - 7, 1), 1, 254)
    scaled = (w * np.exp2(127.0 - byte)[:, None, :]).reshape(k, n).astype(np.float32)
    words = np.ascontiguousarray(scaled.reshape(k // 512, 128, 4, n).transpose(0, 1, 3, 2)).astype(ml_dtypes.float8_e4m3fn).view(np.uint8)
    return words, np.ascontiguousarray(byte.astype(np.uint8).reshape(k // 512, 16, n))


def unpack_weight(words, scales):
    g, p, n, _ = words.shape
    vals = np.ascontiguousarray(words).view(ml_dtypes.float8_e4m3fn).astype(np.float64) * np.repeat(np.exp2(scales.astype(np.float64) - 127.0), 8, axis=1)[..., None]
    return vals.transpose(0, 1, 3, 2).reshape(g * 512, n)

def planes(y):
    n, m = y.shape
    v = y.astype(np.float32).astype(ml_dtypes.bfloat16).astype(np.float64).reshape(n // 32, 32, m)
    top = np.abs(v).max(1)
    byte = np.clip(np.where(top > 0, np.frexp(top)[1] - 1 + 127 - 7, 1), 1, 254)
    codes = (v * np.exp2(127.0 - byte)[:, None, :]).reshape(n, m).astype(np.float32).astype(ml_dtypes.float8_e4m3fn).view(np.uint8)
    words = codes.reshape(n // 512, 128, 4, m).transpose(0, 1, 3, 2)
    return np.ascontiguousarray(words), np.ascontiguousarray(byte.astype(np.uint8).reshape(n // 512, 16, m))


K, T, S, H, W, C = 512, 2048, 512, 512, 384, 512


def setup_inputs():
    n = np.random.standard_normal
    s = mx_kscale(K)[:, None]
    packed_xT = pack_weight(n((K, T)) * s)
    packed_w1 = pack_weight(n((K, H)) / np.sqrt(K) / s)
    return {
        "x_words": packed_xT[0],
        "x_scales": packed_xT[1],
        "w1_words": packed_w1[0],
        "w1_scales": packed_w1[1],
        "gs": (np.random.uniform(0.5, 1.5, (K, 1)) / s).astype(np.float32),
        "offs": striped(np.random.permutation(T)[:S]),
        "n1": striped(np.random.permutation(S)[:W]),
        "n2": striped(np.random.permutation(S)[:W]),
        "ca": striped(np.random.permutation(T)[:C]),
        "cb": striped(np.random.permutation(T)[:C]),
        "n3": striped(np.random.permutation(S)),
        "n4": striped(np.random.permutation(S)),
    }


def reference(x_words, x_scales, w1_words, w1_scales, gs, offs, n1, n2, ca, cb, n3, n4):
    x_ca = unpack_weight(x_words, x_scales)[:, unstriped(ca)]
    xq = unpack_weight(x_words, x_scales)[:, unstriped(offs)]
    y = unpack_weight(w1_words, w1_scales).T @ xq
    old = y[:, unstriped(n1)]
    pa = y[:, unstriped(n2)]
    ra = old - np.tanh(pa)
    ds = y.copy()
    ds[:, unstriped(n1)] = ra
    z = f64(gs) * ds
    zq = mxq(z, 0, "e4m3")
    a = 0.0625 * (x_ca.T @ zq)
    x_cb = unpack_weight(x_words, x_scales)[:, unstriped(cb)]
    b = 0.0625 * (x_cb.T @ zq)
    out_0 = (a - a[:, unstriped(n3)]) / (np.abs(b) + np.abs(b[:, unstriped(n4)]) + 0.5)
    return (out_0,) + planes(out_0)

@@ -1,0 +1,229 @@
+from contextlib import ExitStack
+
+import concourse.mybir as mybir
+
+F32 = mybir.dt.float32
+BF16 = mybir.dt.bfloat16
+I32 = mybir.dt.int32
+U32 = mybir.dt.uint32
+U16 = mybir.dt.uint16
+U8 = mybir.dt.uint8
+FP8X4 = mybir.dt.float8_e4m3fn_x4
+ACT = mybir.ActivationFunctionType
+ALU = mybir.AluOpType
+
+P = 128
+PACK = 4
+T = 2048
+S = 512
+W = 384
+QUADS = 4
+CHUNKS = (256, 128, 128)
+
+FLOPS = 3 * 2 * 512 * 512 * 512
+
+
+def load_scale_rows(queues, plane, scales):
+    for q in range(QUADS):
+        queues[q].dma_start(out=plane[32 * q : 32 * q + 4, :].bitcast(I32), in_=scales[0, 4 * q : 4 * q + 4, :].bitcast(I32))
+
+
+def deal(nc, dst, src, run):
+    nc.vector.tensor_copy(
+        out=dst.rearrange("p (t b i) -> p b t i", t=PACK, i=run),
+        in_=src.rearrange("p (b i t) -> p b t i", t=PACK, i=run),
+    )
+
+
+def tile_picked_ccmpnormbktanh_none_po_kernel(
+    tc, x_words, x_scales, w1_words, w1_scales, gs, offs, n1, n2, ca, cb, n3, n4, out_0, out_1, out_2
+):
+    nc = tc.nc
+    with ExitStack() as ctx:
+        keep = ctx.enter_context(tc.tile_pool(name="keep", bufs=1))
+        psum = ctx.enter_context(tc.psum_pool(name="psum", bufs=1))
+
+        def sb(shape, dtype, name, tag=None):
+            return keep.tile(shape, dtype, name=name, tag=tag or name, align_bytes=64)
+
+        lists = {}
+        for name, src in (("offs", offs), ("n1", n1), ("n2", n2), ("ca", ca), ("cb", cb), ("n3", n3), ("n4", n4)):
+            lists[name] = sb([P, src.shape[1]], U16, "list_" + name)
+
+        xw = sb([P, T], U32, "xw")
+        xs = sb([P, T], U8, "xs")
+        ww = sb([P, S], U32, "ww")
+        ws = sb([P, S], U8, "ws")
+        gain = sb([P, PACK], F32, "gain")
+
+        nc.vector.memset(xs[:, : T // 2].bitcast(I32), 0)
+        nc.gpsimd.memset(xs[:, T // 2 :].bitcast(I32), 0)
+        nc.vector.memset(ws[:].bitcast(I32), 0)
+        nc.sync.dma_start(lists["offs"][:], offs)
+        nc.sync.dma_start(lists["n2"][:], n2)
+        load_scale_rows([nc.sync] * QUADS, xs, x_scales)
+        nc.sync.dma_start(out=xw[:].bitcast(I32), in_=x_words[0].rearrange("p c r -> p (c r)").bitcast(I32))
+        nc.sync.dma_start(out=ww[:].bitcast(I32), in_=w1_words[0].rearrange("p c r -> p (c r)").bitcast(I32))
+        load_scale_rows([nc.sync, nc.sync, nc.gpsimd, nc.gpsimd], ws, w1_scales)
+        nc.sync.dma_start(lists["n1"][:], n1)
+        nc.sync.dma_start(lists["cb"][:], cb)
+        nc.sync.dma_start(out=gain[:], in_=gs.rearrange("(p t) o -> p (t o)", t=PACK))
+        nc.sync.dma_start(lists["ca"][:], ca)
+        nc.sync.dma_start(lists["n4"][:], n4)
+        nc.sync.dma_start(lists["n3"][:], n3)
+
+        def pick(window, name, dtype, tile_name, tag=None):
+            picked = sb([P, S], dtype, tile_name, tag)
+            nc.vector.tensor_copy(picked[:], window[:].indirect(lists[name][:]))
+            return picked
+
+        def dealt_words(src, name):
+            dst = sb([P, S], U32, name)
+            deal(nc, dst[:].bitcast(I32), src[:].bitcast(I32), 4)
+            return dst
+
+        def dealt_bytes(src, name):
+            dst = sb([P, S], U8, name)
+            deal(nc, dst[:], src[:], 16)
+            return dst
+
+        xqs = pick(xs, "offs", U8, "xqs")
+        wsd = dealt_bytes(ws, "wsd")
+        xqw = pick(xw, "offs", U32, "xqw")
+        wwd = sb([P, S], U32, "wwd")
+        ww_by_slot = ww[:].bitcast(I32).rearrange("p (m t) -> p t m", t=PACK)
+        wwd_by_slot = wwd[:].bitcast(I32).rearrange("p (t m) -> p t m", t=PACK)
+        nc.vector.tensor_copy(wwd_by_slot[:, 0:1, :], ww_by_slot[:, 0:1, :])
+        nc.vector.tensor_copy(wwd_by_slot[:, 1:PACK, :], ww_by_slot[:, 1:PACK, :])
+
+        def product(t, words, scales, mov_words, mov_scales, tag):
+            bank = psum.tile([P, S], F32, name=tag, tag=tag)
+            cols = slice(t * P, (t + 1) * P)
+            nc.tensor.matmul_mx(
+                out=bank[:],
+                lhsT=words[:, cols].bitcast(FP8X4),
+                lhsT_scale=scales[:, cols],
+                rhs=mov_words[:].bitcast(FP8X4),
+                rhs_scale=mov_scales[:],
+                start=True,
+                stop=True,
+            )
+            return bank
+
+        ybank = [product(t, wwd, wsd, xqw, xqs, "bank%d" % t) for t in range(PACK)]
+        y = [sb([P, S], F32, "y%d" % t) for t in range(PACK)]
+        old = [sb([P, W], F32, "old%d" % t) for t in range(PACK)]
+        pa = [sb([P, W], F32, "pa%d" % t) for t in range(PACK)]
+        th = [sb([P, W], F32, "th%d" % t) for t in range(PACK)]
+        ra = [sb([P, W], F32, "ra%d" % t) for t in range(PACK)]
+        z = sb([P, S, PACK], BF16, "z")
+        zc = sb([P, PACK - 1, S], BF16, "zc")
+
+        def fetch_old(t):
+            nc.scalar.activation(old[t][:], y[t][:].indirect(lists["n1"][:]), ACT.Copy)
+
+        def fetch_pa(t):
+            nc.vector.tensor_copy(pa[t][:], y[t][:].indirect(lists["n2"][:]))
+
+        def squash(t):
+            nc.scalar.activation(th[t][:], pa[t][:], ACT.Tanh)
+
+        def subtract(t):
+            nc.vector.tensor_tensor(ra[t][:], old[t][:], th[t][:], ALU.subtract)
+
+        def put(t):
+            nc.scalar.activation(y[t][:].indirect(lists["n1"][:]), ra[t][:], ACT.Copy)
+
+        def weigh(t):
+            nc.vector.tensor_scalar(zc[:, t, :], y[t][:], gain[:, t : t + 1], None, ALU.mult)
+
+        nc.scalar.copy(y[0][:], ybank[0][:])
+        fetch_old(0)
+        fetch_pa(0)
+        nc.vector.tensor_copy(y[1][:], ybank[1][:])
+        squash(0)
+        fetch_old(1)
+        subtract(0)
+        put(0)
+        for t in range(1, PACK):
+            fetch_pa(t)
+            if t + 1 < PACK:
+                nc.vector.tensor_copy(y[t + 1][:], ybank[t + 1][:])
+            squash(t)
+            if t + 1 < PACK:
+                fetch_old(t + 1)
+        cbw = pick(xw, "cb", U32, "cbw", "pa0")
+        for t in range(1, PACK):
+            subtract(t)
+        for t in range(1, PACK):
+            put(t)
+        cbs = pick(xs, "cb", U8, "cbs", "pa1")
+        caw = pick(xw, "ca", U32, "caw", "pa2")
+        cas = pick(xs, "ca", U8, "cas", "pa3")
+        weigh(0)
+        cbwd = dealt_words(cbw, "cbwd")
+        cbsd = dealt_bytes(cbs, "cbsd")
+        weigh(1)
+        cawd = dealt_words(caw, "cawd")
+        casd = dealt_bytes(cas, "casd")
+        weigh(2)
+        nc.vector.tensor_copy(
+            out=z[:, :, 0 : PACK - 1].rearrange("p (c i) t -> p c t i", i=4),
+            in_=zc[:].rearrange("p t (c i) -> p c t i", i=4),
+        )
+        nc.vector.tensor_scalar(z[:, :, PACK - 1], y[PACK - 1][:], gain[:, PACK - 1 : PACK], None, ALU.mult)
+        zw = sb([P, S], U32, "zw")
+        zs = sb([P, S], U8, "zs")
+        nc.vector.quantize_mx(out=zw[:].bitcast(FP8X4), scales=zs[:], in_=z[:].rearrange("p j t -> p (j t)"))
+
+        bbank = [product(t, cbwd, cbsd, zw, zs, "bank%d" % (PACK + t)) for t in range(PACK)]
+        abank = [product(t, cawd, casd, zw, zs, "bank%d" % t) for t in range(PACK)]
+        a = sb([P, PACK, S], F32, "a")
+        babs = sb([P, PACK, S], F32, "babs")
+        for t in range(PACK):
+            nc.scalar.activation(babs[:, t, :], bbank[t][:], ACT.Abs)
+        for t in range(PACK):
+            if t < 2:
+                nc.scalar.copy(a[:, t, :], abank[t][:])
+            else:
+                nc.vector.tensor_copy(a[:, t, :], abank[t][:])
+
+        ow = sb([P, S], U32, "ow")
+        osc = sb([P, S], U8, "osc")
+        out_rows = out_0.rearrange("(p t) j -> p t j", t=PACK)
+        out_words = out_1[0].rearrange("p c r -> p (c r)").bitcast(I32)
+        starts = [sum(CHUNKS[:c]) for c in range(len(CHUNKS))]
+        dens = []
+        for c, width in enumerate(CHUNKS):
+            cols = slice(starts[c], starts[c] + width)
+            lcols = slice(starts[c] // 16, (starts[c] + width) // 16)
+            den = sb([P, PACK, width], F32, "den%d" % c)
+            for t in range(PACK):
+                nc.vector.tensor_copy(den[:, t, :], babs[:, t, :].indirect(lists["n4"][:, lcols]))
+            nc.vector.tensor_tensor(den[:], den[:], babs[:, :, cols], ALU.add)
+            dens.append(den)
+        for c, width in enumerate(CHUNKS):
+            cols = slice(starts[c], starts[c] + width)
+            lcols = slice(starts[c] // 16, (starts[c] + width) // 16)
+            num = sb([P, PACK, width], F32, "num%d" % c)
+            for t in range(PACK):
+                nc.scalar.activation(num[:, t, :], a[:, t, :].indirect(lists["n3"][:, lcols]), ACT.Copy)
+            root = sb([P, PACK, width], F32, "root%d" % c)
+            nc.scalar.activation(root[:], dens[c][:], ACT.Abs_reciprocal_sqrt, bias=8.0)
+            nc.scalar.activation(root[:], root[:], ACT.Square)
+            nc.vector.tensor_tensor(num[:], a[:, :, cols], num[:], ALU.subtract)
+            res = sb([P, PACK, width], F32, "res%d" % c)
+            nc.vector.tensor_tensor(res[:], num[:], root[:], ALU.mult)
+            nc.sync.dma_start(out=out_rows[:, :, cols], in_=res[:])
+            woven = sb([P, width, PACK], BF16, "woven%d" % c)
+            nc.vector.tensor_copy(
+                out=woven[:].rearrange("p (c i) t -> p c t i", i=4),
+                in_=res[:].rearrange("p t (c i) -> p c t i", i=4),
+            )
+            nc.vector.quantize_mx(
+                out=ow[:, cols].bitcast(FP8X4), scales=osc[:, cols], in_=woven[:].rearrange("p j t -> p (j t)")
+            )
+            nc.sync.dma_start(out=out_words[:, cols], in_=ow[:, cols].bitcast(I32))
+        for q in range(QUADS):
+            queue = nc.sync if q % 2 == 0 else nc.scalar
+            queue.dma_start(out=out_2[0, 4 * q : 4 * q + 4, :].bitcast(I32), in_=osc[32 * q : 32 * q + 4, :].bitcast(I32))

@@ -1,6 +1,7 @@
 from contextlib import ExitStack
 
 import concourse.mybir as mybir
+from concourse.masks import make_identity
 
 F32 = mybir.dt.float32
 BF16 = mybir.dt.bfloat16
@@ -18,7 +19,8 @@ T = 2048
 S = 512
 W = 384
 QUADS = 4
-CHUNKS = (256, 128, 128)
+CHUNKS = (128, 128, 128, 128)
+HALF = 256
 
 FLOPS = 3 * 2 * 512 * 512 * 512
 
@@ -60,160 +62,202 @@ def tile_picked_ccmpnormbktanh_none_po_kernel(
         nc.gpsimd.memset(xs[:, T // 2 :].bitcast(I32), 0)
         nc.vector.memset(ws[:].bitcast(I32), 0)
         nc.sync.dma_start(lists["offs"][:], offs)
-        nc.sync.dma_start(lists["n2"][:], n2)
+        nc.sync.dma_start(lists["ca"][:], ca)
         load_scale_rows([nc.sync] * QUADS, xs, x_scales)
         nc.sync.dma_start(out=xw[:].bitcast(I32), in_=x_words[0].rearrange("p c r -> p (c r)").bitcast(I32))
         nc.sync.dma_start(out=ww[:].bitcast(I32), in_=w1_words[0].rearrange("p c r -> p (c r)").bitcast(I32))
-        load_scale_rows([nc.sync, nc.sync, nc.gpsimd, nc.gpsimd], ws, w1_scales)
+        load_scale_rows([nc.sync] * QUADS, ws, w1_scales)
+        ident = sb([P, P], F32, "ident")
+        make_identity(nc, ident[:])
         nc.sync.dma_start(lists["n1"][:], n1)
+        nc.sync.dma_start(lists["n2"][:], n2)
         nc.sync.dma_start(lists["cb"][:], cb)
         nc.sync.dma_start(out=gain[:], in_=gs.rearrange("(p t) o -> p (t o)", t=PACK))
-        nc.sync.dma_start(lists["ca"][:], ca)
         nc.sync.dma_start(lists["n4"][:], n4)
         nc.sync.dma_start(lists["n3"][:], n3)
 
-        def pick(window, name, dtype, tile_name, tag=None):
-            picked = sb([P, S], dtype, tile_name, tag)
-            nc.vector.tensor_copy(picked[:], window[:].indirect(lists[name][:]))
+        def pick(window, name, dtype, tile_name, tag=None, part=slice(0, S)):
+            picked = sb([P, part.stop - part.start], dtype, tile_name, tag)
+            nc.vector.tensor_copy(picked[:], window[:].indirect(lists[name][:, part.start // 16 : part.stop // 16]))
             return picked
 
-        def dealt_words(src, name):
-            dst = sb([P, S], U32, name)
+        def dealt_words(src, name, tag=None):
+            dst = sb([P, S], U32, name, tag)
             deal(nc, dst[:].bitcast(I32), src[:].bitcast(I32), 4)
             return dst
 
-        def dealt_bytes(src, name):
-            dst = sb([P, S], U8, name)
+        def dealt_bytes(src, name, tag=None):
+            dst = sb([P, S], U8, name, tag)
             deal(nc, dst[:], src[:], 16)
             return dst
 
         xqs = pick(xs, "offs", U8, "xqs")
-        wsd = dealt_bytes(ws, "wsd")
+        cas = sb([P, S], U8, "cas")
+        nc.vector.tensor_copy(cas[:, 0:HALF], xs[:].indirect(lists["ca"][:, 0:16]))
         xqw = pick(xw, "offs", U32, "xqw")
         wwd = sb([P, S], U32, "wwd")
-        ww_by_slot = ww[:].bitcast(I32).rearrange("p (m t) -> p t m", t=PACK)
-        wwd_by_slot = wwd[:].bitcast(I32).rearrange("p (t m) -> p t m", t=PACK)
-        nc.vector.tensor_copy(wwd_by_slot[:, 0:1, :], ww_by_slot[:, 0:1, :])
-        nc.vector.tensor_copy(wwd_by_slot[:, 1:PACK, :], ww_by_slot[:, 1:PACK, :])
+        wsd = sb([P, S], U8, "wsd")
+        nc.vector.tensor_copy(wwd[:, 0:P].bitcast(I32), ww[:].bitcast(I32)[:, 0::PACK])
+        nc.vector.tensor_copy(wsd[:, 0:P], ws[:, 0::PACK])
+        nc.vector.tensor_copy(
+            wwd[:, P:S].bitcast(I32).rearrange("p (t b i) -> p b t i", t=PACK - 1, i=4),
+            ww[:].bitcast(I32).rearrange("p (b i t) -> p b t i", t=PACK, i=4)[:, :, 1:PACK, :],
+        )
+        nc.vector.tensor_copy(
+            wsd[:, P:S].rearrange("p (t b i) -> p b t i", t=PACK - 1, i=16),
+            ws[:].rearrange("p (b i t) -> p b t i", t=PACK, i=16)[:, :, 1:PACK, :],
+        )
 
-        def product(t, words, scales, mov_words, mov_scales, tag):
-            bank = psum.tile([P, S], F32, name=tag, tag=tag)
+        def product(out, t, words, scales, mov_words, mov_scales):
             cols = slice(t * P, (t + 1) * P)
             nc.tensor.matmul_mx(
-                out=bank[:],
+                out=out,
                 lhsT=words[:, cols].bitcast(FP8X4),
                 lhsT_scale=scales[:, cols],
-                rhs=mov_words[:].bitcast(FP8X4),
-                rhs_scale=mov_scales[:],
+                rhs=mov_words.bitcast(FP8X4),
+                rhs_scale=mov_scales,
                 start=True,
                 stop=True,
             )
-            return bank
 
-        ybank = [product(t, wwd, wsd, xqw, xqs, "bank%d" % t) for t in range(PACK)]
+        def bank(index, shape):
+            return psum.tile(shape, F32, name="bank%d" % index, tag="bank%d" % index)
+
+        ybank = [bank(t, [P, S]) for t in range(PACK)]
+        for t in range(PACK):
+            product(ybank[t][:], t, wwd, wsd, xqw[:], xqs[:])
         y = [sb([P, S], F32, "y%d" % t) for t in range(PACK)]
         old = [sb([P, W], F32, "old%d" % t) for t in range(PACK)]
-        pa = [sb([P, W], F32, "pa%d" % t) for t in range(PACK)]
-        th = [sb([P, W], F32, "th%d" % t) for t in range(PACK)]
+        tneg = [sb([P, S], F32, "tneg%d" % t) for t in range(PACK)]
         ra = [sb([P, W], F32, "ra%d" % t) for t in range(PACK)]
-        z = sb([P, S, PACK], BF16, "z")
+        z = [sb([P, HALF, PACK], BF16, "z%d" % h) for h in range(2)]
         zc = sb([P, PACK - 1, S], BF16, "zc")
 
-        def fetch_old(t):
+        for t in range(PACK):
+            nc.scalar.activation(tneg[t][:], ybank[t][:], ACT.Tanh, scale=-1.0)
+            nc.vector.tensor_copy(y[t][:], ybank[t][:])
+        for t in range(PACK):
             nc.scalar.activation(old[t][:], y[t][:].indirect(lists["n1"][:]), ACT.Copy)
-
-        def fetch_pa(t):
-            nc.vector.tensor_copy(pa[t][:], y[t][:].indirect(lists["n2"][:]))
-
-        def squash(t):
-            nc.scalar.activation(th[t][:], pa[t][:], ACT.Tanh)
-
-        def subtract(t):
-            nc.vector.tensor_tensor(ra[t][:], old[t][:], th[t][:], ALU.subtract)
-
-        def put(t):
+            nc.vector.tensor_tensor(ra[t][:], tneg[t][:].indirect(lists["n2"][:]), old[t][:], ALU.add)
+        for t in range(PACK):
             nc.scalar.activation(y[t][:].indirect(lists["n1"][:]), ra[t][:], ACT.Copy)
 
         def weigh(t):
             nc.vector.tensor_scalar(zc[:, t, :], y[t][:], gain[:, t : t + 1], None, ALU.mult)
 
-        nc.scalar.copy(y[0][:], ybank[0][:])
-        fetch_old(0)
-        fetch_pa(0)
-        nc.vector.tensor_copy(y[1][:], ybank[1][:])
-        squash(0)
-        fetch_old(1)
-        subtract(0)
-        put(0)
-        for t in range(1, PACK):
-            fetch_pa(t)
-            if t + 1 < PACK:
-                nc.vector.tensor_copy(y[t + 1][:], ybank[t + 1][:])
-            squash(t)
-            if t + 1 < PACK:
-                fetch_old(t + 1)
-        cbw = pick(xw, "cb", U32, "cbw", "pa0")
-        for t in range(1, PACK):
-            subtract(t)
-        for t in range(1, PACK):
-            put(t)
-        cbs = pick(xs, "cb", U8, "cbs", "pa1")
-        caw = pick(xw, "ca", U32, "caw", "pa2")
-        cas = pick(xs, "ca", U8, "cas", "pa3")
+        cbw = pick(xw, "cb", U32, "cbw", "tneg0")
+        cbs = pick(xs, "cb", U8, "cbs", "tneg1")
+        caw = pick(xw, "ca", U32, "caw", "tneg2")
+        cas1 = pick(xs, "ca", U8, "cas1", "tneg3", slice(HALF, S))
         weigh(0)
         cbwd = dealt_words(cbw, "cbwd")
         cbsd = dealt_bytes(cbs, "cbsd")
         weigh(1)
-        cawd = dealt_words(caw, "cawd")
-        casd = dealt_bytes(cas, "casd")
         weigh(2)
-        nc.vector.tensor_copy(
-            out=z[:, :, 0 : PACK - 1].rearrange("p (c i) t -> p c t i", i=4),
-            in_=zc[:].rearrange("p t (c i) -> p c t i", i=4),
-        )
-        nc.vector.tensor_scalar(z[:, :, PACK - 1], y[PACK - 1][:], gain[:, PACK - 1 : PACK], None, ALU.mult)
+        halves = [slice(0, HALF), slice(HALF, S)]
+        for h, cols in enumerate(halves):
+            nc.vector.tensor_copy(
+                out=z[h][:, :, 0 : PACK - 1].rearrange("p (c i) t -> p c t i", i=4),
+                in_=zc[:, :, cols].rearrange("p t (c i) -> p c t i", i=4),
+            )
         zw = sb([P, S], U32, "zw")
         zs = sb([P, S], U8, "zs")
-        nc.vector.quantize_mx(out=zw[:].bitcast(FP8X4), scales=zs[:], in_=z[:].rearrange("p j t -> p (j t)"))
+        for h, cols in enumerate(halves):
+            nc.vector.tensor_scalar(z[h][:, :, PACK - 1], y[PACK - 1][:, cols], gain[:, PACK - 1 : PACK], None, ALU.mult)
+            nc.vector.quantize_mx(
+                out=zw[:, cols].bitcast(FP8X4), scales=zs[:, cols], in_=z[h][:].rearrange("p j t -> p (j t)")
+            )
+        warm = sb([P, 1], F32, "warm")
+        nc.scalar.activation(warm[:], y[PACK - 1][:, 0:1], ACT.Abs_reciprocal_sqrt, bias=8.0, scale=0.0)
+        cawd = dealt_words(caw, "cawd", "z0")
+        casd = sb([P, S], U8, "casd", "z1")
+        casd_by_slot = casd[:].rearrange("p (t m) -> p t m", t=PACK)
+        for h, part in enumerate((cas[:, 0:HALF], cas1[:])):
+            nc.vector.tensor_copy(
+                casd_by_slot[:, :, h * 64 : (h + 1) * 64].rearrange("p t (b i) -> p b t i", i=16),
+                part.rearrange("p (b i t) -> p b t i", t=PACK, i=16),
+            )
 
-        bbank = [product(t, cbwd, cbsd, zw, zs, "bank%d" % (PACK + t)) for t in range(PACK)]
-        abank = [product(t, cawd, casd, zw, zs, "bank%d" % t) for t in range(PACK)]
+        def scores(first_bank, words, scales, order):
+            made = []
+            for index, (pair, h) in enumerate(order):
+                sums = bank(first_bank + index, [P, 2, HALF])
+                for u in range(2):
+                    product(sums[:, u, :], 2 * pair + u, words, scales, zw[:, halves[h]], zs[:, halves[h]])
+                made.append((pair, h, sums))
+            return made
+
+        bsums = scores(PACK, cbwd, cbsd, ((0, 0), (1, 0), (0, 1), (1, 1)))
+        asums = scores(0, cawd, casd, ((0, 0), (0, 1), (1, 0), (1, 1)))
         a = sb([P, PACK, S], F32, "a")
         babs = sb([P, PACK, S], F32, "babs")
-        for t in range(PACK):
-            nc.scalar.activation(babs[:, t, :], bbank[t][:], ACT.Abs)
-        for t in range(PACK):
-            if t < 2:
-                nc.scalar.copy(a[:, t, :], abank[t][:])
-            else:
-                nc.vector.tensor_copy(a[:, t, :], abank[t][:])
+        for pair, h, sums in bsums:
+            nc.scalar.activation(babs[:, 2 * pair : 2 * pair + 2, halves[h]], sums[:], ACT.Abs)
+        def leave_a(index, engine_copy):
+            pair, h, sums = asums[index]
+            engine_copy(a[:, 2 * pair : 2 * pair + 2, halves[h]], sums[:])
 
         ow = sb([P, S], U32, "ow")
         osc = sb([P, S], U8, "osc")
         out_rows = out_0.rearrange("(p t) j -> p t j", t=PACK)
         out_words = out_1[0].rearrange("p c r -> p (c r)").bitcast(I32)
         starts = [sum(CHUNKS[:c]) for c in range(len(CHUNKS))]
-        dens = []
-        for c, width in enumerate(CHUNKS):
-            cols = slice(starts[c], starts[c] + width)
-            lcols = slice(starts[c] // 16, (starts[c] + width) // 16)
-            den = sb([P, PACK, width], F32, "den%d" % c)
+        roots = [sb([P, PACK, P], F32, "root%d" % block) for block in range(S // P)]
+        nums = {}
+        dens = {}
+        inverse = {}
+
+        def fetch_far(h):
+            far = sb([P, PACK, HALF], F32, "far%d" % h)
             for t in range(PACK):
-                nc.vector.tensor_copy(den[:, t, :], babs[:, t, :].indirect(lists["n4"][:, lcols]))
-            nc.vector.tensor_tensor(den[:], den[:], babs[:, :, cols], ALU.add)
-            dens.append(den)
-        for c, width in enumerate(CHUNKS):
-            cols = slice(starts[c], starts[c] + width)
-            lcols = slice(starts[c] // 16, (starts[c] + width) // 16)
-            num = sb([P, PACK, width], F32, "num%d" % c)
+                nc.vector.tensor_copy(far[:, t, :], babs[:, t, :].indirect(lists["n4"][:, 16 * h : 16 * (h + 1)]))
+            for u in range(2):
+                for t in range(PACK):
+                    nc.tensor.matmul(
+                        dens[2 * h + u][:, t, :], far[:, t, u * P : (u + 1) * P], ident[:],
+                        start=False, stop=(t == PACK - 1), is_transpose=True,
+                    )
+
+        def turn_near(block):
+            dens[block] = bank(PACK + block, [P, PACK, P])
             for t in range(PACK):
-                nc.scalar.activation(num[:, t, :], a[:, t, :].indirect(lists["n3"][:, lcols]), ACT.Copy)
-            root = sb([P, PACK, width], F32, "root%d" % c)
-            nc.scalar.activation(root[:], dens[c][:], ACT.Abs_reciprocal_sqrt, bias=8.0)
-            nc.scalar.activation(root[:], root[:], ACT.Square)
-            nc.vector.tensor_tensor(num[:], a[:, :, cols], num[:], ALU.subtract)
+                nc.tensor.matmul(
+                    dens[block][:, t, :], babs[:, t, block * P : (block + 1) * P], ident[:],
+                    start=(t == 0), stop=False, is_transpose=True,
+                )
+
+        def invert(block):
+            root = roots[block]
+            nc.scalar.activation(root[:], dens[block][:], ACT.Abs_reciprocal_sqrt, bias=8.0)
+            nc.gpsimd.tensor_tensor(root[:], root[:], root[:], ALU.mult)
+            inverse[block] = bank(PACK + block, [P, PACK, P])
+            for t in range(PACK):
+                nc.tensor.transpose(inverse[block][:, t, :], root[:, t, :], ident[:])
+
+        def fetch_a(c, pair):
+            lcols = slice(starts[c] // 16, (starts[c] + CHUNKS[c]) // 16)
+            if pair == 0:
+                nums[c] = sb([P, PACK, CHUNKS[c]], F32, "num%d" % c, (None, "far0", "far1", "root0")[c])
+            for t in (2 * pair, 2 * pair + 1):
+                nc.scalar.activation(nums[c][:, t, :], a[:, t, :].indirect(lists["n3"][:, lcols]), ACT.Copy)
+
+        def subtract(c, pair):
+            h, inside = divmod(starts[c], HALF)
+            rows = slice(2 * pair, 2 * pair + 2)
+            near = asums[2 * pair + h][2][:, :, inside : inside + CHUNKS[c]]
+            nc.vector.tensor_tensor(nums[c][:, rows, :], near, nums[c][:, rows, :], ALU.subtract)
+
+        def finish(c):
+            width = CHUNKS[c]
+            cols = slice(starts[c], starts[c] + width)
+            num = nums[c]
             res = sb([P, PACK, width], F32, "res%d" % c)
-            nc.vector.tensor_tensor(res[:], num[:], root[:], ALU.mult)
+            for first in range(0, width, P):
+                last = min(first + P, width)
+                block, inside = divmod(starts[c] + first, P)
+                nc.vector.tensor_tensor(
+                    res[:, :, first:last], inverse[block][:, :, inside : inside + last - first], num[:, :, first:last], ALU.mult
+                )
             nc.sync.dma_start(out=out_rows[:, :, cols], in_=res[:])
             woven = sb([P, width, PACK], BF16, "woven%d" % c)
             nc.vector.tensor_copy(
@@ -224,6 +268,41 @@ def tile_picked_ccmpnormbktanh_none_po_kernel(
                 out=ow[:, cols].bitcast(FP8X4), scales=osc[:, cols], in_=woven[:].rearrange("p j t -> p (j t)")
             )
             nc.sync.dma_start(out=out_words[:, cols], in_=ow[:, cols].bitcast(I32))
+
+        turn_near(0)
+        turn_near(1)
+        fetch_far(0)
+        turn_near(2)
+        turn_near(3)
+        leave_a(0, nc.scalar.copy)
+        leave_a(1, nc.scalar.copy)
+        leave_a(2, nc.scalar.copy)
+        leave_a(3, nc.scalar.copy)
+        fetch_a(0, 0)
+        fetch_a(0, 1)
+        invert(0)
+        invert(1)
+        fetch_far(1)
+        subtract(0, 0)
+        subtract(0, 1)
+        finish(0)
+        fetch_a(1, 0)
+        fetch_a(1, 1)
+        invert(2)
+        invert(3)
+        subtract(1, 0)
+        subtract(1, 1)
+        finish(1)
+        fetch_a(2, 0)
+        fetch_a(2, 1)
+        subtract(2, 0)
+        subtract(2, 1)
+        finish(2)
+        fetch_a(3, 0)
+        fetch_a(3, 1)
+        subtract(3, 0)
+        subtract(3, 1)
+        finish(3)
         for q in range(QUADS):
             queue = nc.sync if q % 2 == 0 else nc.scalar
             queue.dma_start(out=out_2[0, 4 * q : 4 * q + 4, :].bitcast(I32), in_=osc[32 * q : 32 * q + 4, :].bitcast(I32))

@@ -151,9 +151,9 @@ def tile_picked_ccmpnormbktanh_none_po_kernel(
         cas1 = pick(xs, "ca", U8, "cas1", "tneg3", slice(HALF, S))
         weigh(0)
         cbwd = dealt_words(cbw, "cbwd")
-        cbsd = dealt_bytes(cbs, "cbsd")
         weigh(1)
         weigh(2)
+        cbsd = dealt_bytes(cbs, "cbsd")
         halves = [slice(0, HALF), slice(HALF, S)]
         for h, cols in enumerate(halves):
             nc.vector.tensor_copy(
@@ -178,17 +178,20 @@ def tile_picked_ccmpnormbktanh_none_po_kernel(
                 part.rearrange("p (b i t) -> p b t i", t=PACK, i=16),
             )
 
-        def scores(first_bank, words, scales, order):
-            made = []
-            for index, (pair, h) in enumerate(order):
-                sums = bank(first_bank + index, [P, 2, HALF])
-                for u in range(2):
-                    product(sums[:, u, :], 2 * pair + u, words, scales, zw[:, halves[h]], zs[:, halves[h]])
-                made.append((pair, h, sums))
-            return made
+        def scores(bank_index, words, scales, index):
+            pair, h = divmod(index, 2)
+            sums = bank(bank_index, [P, 2, HALF])
+            for u in range(2):
+                product(sums[:, u, :], 2 * pair + u, words, scales, zw[:, halves[h]], zs[:, halves[h]])
+            return pair, h, sums
 
-        bsums = scores(PACK, cbwd, cbsd, ((0, 0), (1, 0), (0, 1), (1, 1)))
-        asums = scores(0, cawd, casd, ((0, 0), (0, 1), (1, 0), (1, 1)))
+        bsums = []
+        asums = []
+        for kind, index in (("b", 0), ("b", 1), ("b", 2), ("b", 3), ("a", 0), ("a", 1), ("a", 2), ("a", 3)):
+            if kind == "b":
+                bsums.append(scores(PACK + index, cbwd, cbsd, index))
+            else:
+                asums.append(scores(index, cawd, casd, index))
         a = sb([P, PACK, S], F32, "a")
         babs = sb([P, PACK, S], F32, "babs")
         for pair, h, sums in bsums:
@@ -205,16 +208,20 @@ def tile_picked_ccmpnormbktanh_none_po_kernel(
         roots = [sb([P, PACK, P], F32, "root%d" % block) for block in range(S // P)]
         nums = {}
         dens = {}
+        fars = {}
         inverse = {}
 
         def fetch_far(h):
-            far = sb([P, PACK, HALF], F32, "far%d" % h)
+            far = sb([P, PACK, HALF], F32, "far%d" % h, (None, "z0")[h])
             for t in range(PACK):
                 nc.vector.tensor_copy(far[:, t, :], babs[:, t, :].indirect(lists["n4"][:, 16 * h : 16 * (h + 1)]))
-            for u in range(2):
-                for t in range(PACK):
+            fars[h] = far
+
+        def turn_far(h):
+            for t in range(PACK):
+                for u in range(2):
                     nc.tensor.matmul(
-                        dens[2 * h + u][:, t, :], far[:, t, u * P : (u + 1) * P], ident[:],
+                        dens[2 * h + u][:, t, :], fars[h][:, t, u * P : (u + 1) * P], ident[:],
                         start=False, stop=(t == PACK - 1), is_transpose=True,
                     )
 
@@ -229,7 +236,10 @@ def tile_picked_ccmpnormbktanh_none_po_kernel(
         def invert(block):
             root = roots[block]
             nc.scalar.activation(root[:], dens[block][:], ACT.Abs_reciprocal_sqrt, bias=8.0)
-            nc.gpsimd.tensor_tensor(root[:], root[:], root[:], ALU.mult)
+            if block in (0, 1):
+                nc.gpsimd.tensor_tensor(root[:], root[:], root[:], ALU.mult)
+            else:
+                nc.scalar.activation(root[:], root[:], ACT.Square)
             inverse[block] = bank(PACK + block, [P, PACK, P])
             for t in range(PACK):
                 nc.tensor.transpose(inverse[block][:, t, :], root[:, t, :], ident[:])
@@ -237,7 +247,7 @@ def tile_picked_ccmpnormbktanh_none_po_kernel(
         def fetch_a(c, pair):
             lcols = slice(starts[c] // 16, (starts[c] + CHUNKS[c]) // 16)
             if pair == 0:
-                nums[c] = sb([P, PACK, CHUNKS[c]], F32, "num%d" % c, (None, "far0", "far1", "root0")[c])
+                nums[c] = sb([P, PACK, CHUNKS[c]], F32, "num%d" % c, (None, "far0", "z0", "root0")[c])
             for t in (2 * pair, 2 * pair + 1):
                 nc.scalar.activation(nums[c][:, t, :], a[:, t, :].indirect(lists["n3"][:, lcols]), ACT.Copy)
 
@@ -247,7 +257,9 @@ def tile_picked_ccmpnormbktanh_none_po_kernel(
             near = asums[2 * pair + h][2][:, :, inside : inside + CHUNKS[c]]
             nc.vector.tensor_tensor(nums[c][:, rows, :], near, nums[c][:, rows, :], ALU.subtract)
 
-        def finish(c):
+        results = {}
+
+        def multiply(c):
             width = CHUNKS[c]
             cols = slice(starts[c], starts[c] + width)
             num = nums[c]
@@ -259,50 +271,50 @@ def tile_picked_ccmpnormbktanh_none_po_kernel(
                     res[:, :, first:last], inverse[block][:, :, inside : inside + last - first], num[:, :, first:last], ALU.mult
                 )
             nc.sync.dma_start(out=out_rows[:, :, cols], in_=res[:])
+            results[c] = res
+
+        def hand_on(c, on_gpsimd):
+            width = CHUNKS[c]
+            cols = slice(starts[c], starts[c] + width)
             woven = sb([P, width, PACK], BF16, "woven%d" % c)
-            nc.vector.tensor_copy(
-                out=woven[:].rearrange("p (c i) t -> p c t i", i=4),
-                in_=res[:].rearrange("p t (c i) -> p c t i", i=4),
-            )
+            dst = woven[:].rearrange("p (c i) t -> p c t i", i=4)
+            src = results[c][:].rearrange("p t (c i) -> p c t i", i=4)
+            if on_gpsimd:
+                nc.gpsimd.tensor_scalar(dst, src, 1.0, 0.0, ALU.mult, ALU.add)
+            else:
+                nc.vector.tensor_copy(out=dst, in_=src)
             nc.vector.quantize_mx(
                 out=ow[:, cols].bitcast(FP8X4), scales=osc[:, cols], in_=woven[:].rearrange("p j t -> p (j t)")
             )
             nc.sync.dma_start(out=out_words[:, cols], in_=ow[:, cols].bitcast(I32))
 
-        turn_near(0)
-        turn_near(1)
-        fetch_far(0)
-        turn_near(2)
-        turn_near(3)
         leave_a(0, nc.scalar.copy)
         leave_a(1, nc.scalar.copy)
-        leave_a(2, nc.scalar.copy)
-        leave_a(3, nc.scalar.copy)
+        fetch_far(0)
+        turn_near(0)
+        turn_near(1)
+        turn_far(0)
         fetch_a(0, 0)
-        fetch_a(0, 1)
+        leave_a(2, nc.scalar.copy)
         invert(0)
+        leave_a(3, nc.vector.tensor_copy)
+        fetch_a(0, 1)
         invert(1)
         fetch_far(1)
-        subtract(0, 0)
-        subtract(0, 1)
-        finish(0)
-        fetch_a(1, 0)
-        fetch_a(1, 1)
+        turn_near(2)
+        turn_near(3)
+        turn_far(1)
         invert(2)
         invert(3)
-        subtract(1, 0)
-        subtract(1, 1)
-        finish(1)
-        fetch_a(2, 0)
-        fetch_a(2, 1)
-        subtract(2, 0)
-        subtract(2, 1)
-        finish(2)
-        fetch_a(3, 0)
-        fetch_a(3, 1)
-        subtract(3, 0)
-        subtract(3, 1)
-        finish(3)
+        for c in range(len(CHUNKS)):
+            if c > 0:
+                fetch_a(c, 0)
+                fetch_a(c, 1)
+            pass
+            subtract(c, 0)
+            subtract(c, 1)
+            multiply(c)
+            hand_on(c, False)
         for q in range(QUADS):
             queue = nc.sync if q % 2 == 0 else nc.scalar
             queue.dma_start(out=out_2[0, 4 * q : 4 * q + 4, :].bitcast(I32), in_=osc[32 * q : 32 * q + 4, :].bitcast(I32))

@@ -236,9 +236,9 @@ def tile_picked_ccmpnormbktanh_none_po_kernel(
         def invert(block):
             root = roots[block]
             nc.scalar.activation(root[:], dens[block][:], ACT.Abs_reciprocal_sqrt, bias=8.0)
-            if block in (0, 1):
+            if block in ():
                 nc.gpsimd.tensor_tensor(root[:], root[:], root[:], ALU.mult)
-            else:
+            elif block not in (0, 1):
                 nc.scalar.activation(root[:], root[:], ACT.Square)
             inverse[block] = bank(PACK + block, [P, PACK, P])
             for t in range(PACK):
@@ -270,6 +270,8 @@ def tile_picked_ccmpnormbktanh_none_po_kernel(
                 nc.vector.tensor_tensor(
                     res[:, :, first:last], inverse[block][:, :, inside : inside + last - first], num[:, :, first:last], ALU.mult
                 )
+            if block in (0, 1):
+                nc.vector.tensor_tensor(res[:], inverse[block][:, :, inside : inside + width], res[:], ALU.mult)
             nc.sync.dma_start(out=out_rows[:, :, cols], in_=res[:])
             results[c] = res
 
@@ -304,13 +306,12 @@ def tile_picked_ccmpnormbktanh_none_po_kernel(
         turn_near(2)
         turn_near(3)
         turn_far(1)
-        invert(2)
-        invert(3)
         for c in range(len(CHUNKS)):
             if c > 0:
                 fetch_a(c, 0)
                 fetch_a(c, 1)
-            pass
+            if c in (1, 2):
+                invert(c + 1)
             subtract(c, 0)
             subtract(c, 1)
             multiply(c)

from contextlib import ExitStack

import concourse.mybir as mybir
from concourse.masks import make_identity

F32 = mybir.dt.float32
BF16 = mybir.dt.bfloat16
I32 = mybir.dt.int32
U32 = mybir.dt.uint32
U16 = mybir.dt.uint16
U8 = mybir.dt.uint8
FP8X4 = mybir.dt.float8_e4m3fn_x4
ACT = mybir.ActivationFunctionType
ALU = mybir.AluOpType

P = 128
PACK = 4
T = 2048
S = 512
W = 384
QUADS = 4
CHUNKS = (128, 128, 128, 128)
HALF = 256

FLOPS = 3 * 2 * 512 * 512 * 512


def load_scale_rows(queues, plane, scales):
    for q in range(QUADS):
        queues[q].dma_start(out=plane[32 * q : 32 * q + 4, :].bitcast(I32), in_=scales[0, 4 * q : 4 * q + 4, :].bitcast(I32))


def deal(nc, dst, src, run):
    nc.vector.tensor_copy(
        out=dst.rearrange("p (t b i) -> p b t i", t=PACK, i=run),
        in_=src.rearrange("p (b i t) -> p b t i", t=PACK, i=run),
    )


def tile_picked_ccmpnormbktanh_none_po_kernel(
    tc, x_words, x_scales, w1_words, w1_scales, gs, offs, n1, n2, ca, cb, n3, n4, out_0, out_1, out_2
):
    nc = tc.nc
    with ExitStack() as ctx:
        keep = ctx.enter_context(tc.tile_pool(name="keep", bufs=1))
        psum = ctx.enter_context(tc.psum_pool(name="psum", bufs=1))

        def sb(shape, dtype, name, tag=None):
            return keep.tile(shape, dtype, name=name, tag=tag or name, align_bytes=64)

        lists = {}
        for name, src in (("offs", offs), ("n1", n1), ("n2", n2), ("ca", ca), ("cb", cb), ("n3", n3), ("n4", n4)):
            lists[name] = sb([P, src.shape[1]], U16, "list_" + name)

        xw = sb([P, T], U32, "xw")
        xs = sb([P, T], U8, "xs")
        ww = sb([P, S], U32, "ww")
        ws = sb([P, S], U8, "ws")
        gain = sb([P, PACK], F32, "gain")

        nc.vector.memset(xs[:, : T // 2].bitcast(I32), 0)
        nc.gpsimd.memset(xs[:, T // 2 :].bitcast(I32), 0)
        nc.vector.memset(ws[:].bitcast(I32), 0)
        nc.sync.dma_start(lists["offs"][:], offs)
        nc.sync.dma_start(lists["ca"][:], ca)
        load_scale_rows([nc.sync] * QUADS, xs, x_scales)
        nc.sync.dma_start(out=xw[:].bitcast(I32), in_=x_words[0].rearrange("p c r -> p (c r)").bitcast(I32))
        nc.sync.dma_start(out=ww[:].bitcast(I32), in_=w1_words[0].rearrange("p c r -> p (c r)").bitcast(I32))
        load_scale_rows([nc.sync] * QUADS, ws, w1_scales)
        ident = sb([P, P], F32, "ident")
        make_identity(nc, ident[:])
        nc.sync.dma_start(lists["n1"][:], n1)
        nc.sync.dma_start(lists["n2"][:], n2)
        nc.sync.dma_start(lists["cb"][:], cb)
        nc.sync.dma_start(out=gain[:], in_=gs.rearrange("(p t) o -> p (t o)", t=PACK))
        nc.sync.dma_start(lists["n4"][:], n4)
        nc.sync.dma_start(lists["n3"][:], n3)

        def pick(window, name, dtype, tile_name, tag=None, part=slice(0, S)):
            picked = sb([P, part.stop - part.start], dtype, tile_name, tag)
            nc.vector.tensor_copy(picked[:], window[:].indirect(lists[name][:, part.start // 16 : part.stop // 16]))
            return picked

        def dealt_words(src, name, tag=None):
            dst = sb([P, S], U32, name, tag)
            deal(nc, dst[:].bitcast(I32), src[:].bitcast(I32), 4)
            return dst

        def dealt_bytes(src, name, tag=None):
            dst = sb([P, S], U8, name, tag)
            deal(nc, dst[:], src[:], 16)
            return dst

        xqs = pick(xs, "offs", U8, "xqs")
        cas = sb([P, S], U8, "cas")
        nc.vector.tensor_copy(cas[:, 0:HALF], xs[:].indirect(lists["ca"][:, 0:16]))
        xqw = pick(xw, "offs", U32, "xqw")
        wwd = sb([P, S], U32, "wwd")
        wsd = sb([P, S], U8, "wsd")
        nc.vector.tensor_copy(wwd[:, 0:P].bitcast(I32), ww[:].bitcast(I32)[:, 0::PACK])
        nc.vector.tensor_copy(wsd[:, 0:P], ws[:, 0::PACK])
        nc.vector.tensor_copy(
            wwd[:, P:S].bitcast(I32).rearrange("p (t b i) -> p b t i", t=PACK - 1, i=4),
            ww[:].bitcast(I32).rearrange("p (b i t) -> p b t i", t=PACK, i=4)[:, :, 1:PACK, :],
        )
        nc.vector.tensor_copy(
            wsd[:, P:S].rearrange("p (t b i) -> p b t i", t=PACK - 1, i=16),
            ws[:].rearrange("p (b i t) -> p b t i", t=PACK, i=16)[:, :, 1:PACK, :],
        )

        def product(out, t, words, scales, mov_words, mov_scales):
            cols = slice(t * P, (t + 1) * P)
            nc.tensor.matmul_mx(
                out=out,
                lhsT=words[:, cols].bitcast(FP8X4),
                lhsT_scale=scales[:, cols],
                rhs=mov_words.bitcast(FP8X4),
                rhs_scale=mov_scales,
                start=True,
                stop=True,
            )

        def bank(index, shape):
            return psum.tile(shape, F32, name="bank%d" % index, tag="bank%d" % index)

        ybank = [bank(t, [P, S]) for t in range(PACK)]
        for t in range(PACK):
            product(ybank[t][:], t, wwd, wsd, xqw[:], xqs[:])
        y = [sb([P, S], F32, "y%d" % t) for t in range(PACK)]
        old = [sb([P, W], F32, "old%d" % t) for t in range(PACK)]
        tneg = [sb([P, S], F32, "tneg%d" % t) for t in range(PACK)]
        ra = [sb([P, W], F32, "ra%d" % t) for t in range(PACK)]
        z = [sb([P, HALF, PACK], BF16, "z%d" % h) for h in range(2)]
        zc = sb([P, PACK - 1, S], BF16, "zc")

        for t in range(PACK):
            nc.scalar.activation(tneg[t][:], ybank[t][:], ACT.Tanh, scale=-1.0)
            nc.vector.tensor_copy(y[t][:], ybank[t][:])
        for t in range(PACK):
            nc.scalar.activation(old[t][:], y[t][:].indirect(lists["n1"][:]), ACT.Copy)
            nc.vector.tensor_tensor(ra[t][:], tneg[t][:].indirect(lists["n2"][:]), old[t][:], ALU.add)
        for t in range(PACK):
            nc.scalar.activation(y[t][:].indirect(lists["n1"][:]), ra[t][:], ACT.Copy)

        def weigh(t):
            nc.vector.tensor_scalar(zc[:, t, :], y[t][:], gain[:, t : t + 1], None, ALU.mult)

        cbw = pick(xw, "cb", U32, "cbw", "tneg0")
        cbs = pick(xs, "cb", U8, "cbs", "tneg1")
        caw = pick(xw, "ca", U32, "caw", "tneg2")
        cas1 = pick(xs, "ca", U8, "cas1", "tneg3", slice(HALF, S))
        weigh(0)
        cbwd = dealt_words(cbw, "cbwd")
        weigh(1)
        weigh(2)
        cbsd = dealt_bytes(cbs, "cbsd")
        halves = [slice(0, HALF), slice(HALF, S)]
        for h, cols in enumerate(halves):
            nc.vector.tensor_copy(
                out=z[h][:, :, 0 : PACK - 1].rearrange("p (c i) t -> p c t i", i=4),
                in_=zc[:, :, cols].rearrange("p t (c i) -> p c t i", i=4),
            )
        zw = sb([P, S], U32, "zw")
        zs = sb([P, S], U8, "zs")
        for h, cols in enumerate(halves):
            nc.vector.tensor_scalar(z[h][:, :, PACK - 1], y[PACK - 1][:, cols], gain[:, PACK - 1 : PACK], None, ALU.mult)
            nc.vector.quantize_mx(
                out=zw[:, cols].bitcast(FP8X4), scales=zs[:, cols], in_=z[h][:].rearrange("p j t -> p (j t)")
            )
        warm = sb([P, 1], F32, "warm")
        nc.scalar.activation(warm[:], y[PACK - 1][:, 0:1], ACT.Abs_reciprocal_sqrt, bias=8.0, scale=0.0)
        cawd = dealt_words(caw, "cawd", "z0")
        casd = sb([P, S], U8, "casd", "z1")
        casd_by_slot = casd[:].rearrange("p (t m) -> p t m", t=PACK)
        for h, part in enumerate((cas[:, 0:HALF], cas1[:])):
            nc.vector.tensor_copy(
                casd_by_slot[:, :, h * 64 : (h + 1) * 64].rearrange("p t (b i) -> p b t i", i=16),
                part.rearrange("p (b i t) -> p b t i", t=PACK, i=16),
            )

        def scores(bank_index, words, scales, index):
            pair, h = divmod(index, 2)
            sums = bank(bank_index, [P, 2, HALF])
            for u in range(2):
                product(sums[:, u, :], 2 * pair + u, words, scales, zw[:, halves[h]], zs[:, halves[h]])
            return pair, h, sums

        bsums = []
        asums = []
        for kind, index in (("b", 0), ("b", 1), ("b", 2), ("b", 3), ("a", 0), ("a", 1), ("a", 2), ("a", 3)):
            if kind == "b":
                bsums.append(scores(PACK + index, cbwd, cbsd, index))
            else:
                asums.append(scores(index, cawd, casd, index))
        a = sb([P, PACK, S], F32, "a")
        babs = sb([P, PACK, S], F32, "babs")
        for pair, h, sums in bsums:
            nc.scalar.activation(babs[:, 2 * pair : 2 * pair + 2, halves[h]], sums[:], ACT.Abs)
        def leave_a(index, engine_copy):
            pair, h, sums = asums[index]
            engine_copy(a[:, 2 * pair : 2 * pair + 2, halves[h]], sums[:])

        ow = sb([P, S], U32, "ow")
        osc = sb([P, S], U8, "osc")
        out_rows = out_0.rearrange("(p t) j -> p t j", t=PACK)
        out_words = out_1[0].rearrange("p c r -> p (c r)").bitcast(I32)
        starts = [sum(CHUNKS[:c]) for c in range(len(CHUNKS))]
        roots = [sb([P, PACK, P], F32, "root%d" % block) for block in range(S // P)]
        nums = {}
        dens = {}
        fars = {}
        inverse = {}

        def fetch_far(h):
            far = sb([P, PACK, HALF], F32, "far%d" % h, (None, "z0")[h])
            for t in range(PACK):
                nc.vector.tensor_copy(far[:, t, :], babs[:, t, :].indirect(lists["n4"][:, 16 * h : 16 * (h + 1)]))
            fars[h] = far

        def turn_far(h):
            for t in range(PACK):
                for u in range(2):
                    nc.tensor.matmul(
                        dens[2 * h + u][:, t, :], fars[h][:, t, u * P : (u + 1) * P], ident[:],
                        start=False, stop=(t == PACK - 1), is_transpose=True,
                    )

        def turn_near(block):
            dens[block] = bank(PACK + block, [P, PACK, P])
            for t in range(PACK):
                nc.tensor.matmul(
                    dens[block][:, t, :], babs[:, t, block * P : (block + 1) * P], ident[:],
                    start=(t == 0), stop=False, is_transpose=True,
                )

        def invert(block):
            root = roots[block]
            nc.scalar.activation(root[:], dens[block][:], ACT.Abs_reciprocal_sqrt, bias=8.0)
            if block in ():
                nc.gpsimd.tensor_tensor(root[:], root[:], root[:], ALU.mult)
            elif block not in (0, 1):
                nc.scalar.activation(root[:], root[:], ACT.Square)
            inverse[block] = bank(PACK + block, [P, PACK, P])
            for t in range(PACK):
                nc.tensor.transpose(inverse[block][:, t, :], root[:, t, :], ident[:])

        def fetch_a(c, pair):
            lcols = slice(starts[c] // 16, (starts[c] + CHUNKS[c]) // 16)
            if pair == 0:
                nums[c] = sb([P, PACK, CHUNKS[c]], F32, "num%d" % c, (None, "far0", "z0", "root0")[c])
            for t in (2 * pair, 2 * pair + 1):
                nc.scalar.activation(nums[c][:, t, :], a[:, t, :].indirect(lists["n3"][:, lcols]), ACT.Copy)

        def subtract(c, pair):
            h, inside = divmod(starts[c], HALF)
            rows = slice(2 * pair, 2 * pair + 2)
            near = asums[2 * pair + h][2][:, :, inside : inside + CHUNKS[c]]
            nc.vector.tensor_tensor(nums[c][:, rows, :], near, nums[c][:, rows, :], ALU.subtract)

        results = {}

        def multiply(c):
            width = CHUNKS[c]
            cols = slice(starts[c], starts[c] + width)
            num = nums[c]
            res = sb([P, PACK, width], F32, "res%d" % c)
            for first in range(0, width, P):
                last = min(first + P, width)
                block, inside = divmod(starts[c] + first, P)
                nc.vector.tensor_tensor(
                    res[:, :, first:last], inverse[block][:, :, inside : inside + last - first], num[:, :, first:last], ALU.mult
                )
            if block in (0, 1):
                nc.vector.tensor_tensor(res[:], inverse[block][:, :, inside : inside + width], res[:], ALU.mult)
            nc.sync.dma_start(out=out_rows[:, :, cols], in_=res[:])
            results[c] = res

        def hand_on(c, on_gpsimd):
            width = CHUNKS[c]
            cols = slice(starts[c], starts[c] + width)
            woven = sb([P, width, PACK], BF16, "woven%d" % c)
            dst = woven[:].rearrange("p (c i) t -> p c t i", i=4)
            src = results[c][:].rearrange("p t (c i) -> p c t i", i=4)
            if on_gpsimd:
                nc.gpsimd.tensor_scalar(dst, src, 1.0, 0.0, ALU.mult, ALU.add)
            else:
                nc.vector.tensor_copy(out=dst, in_=src)
            nc.vector.quantize_mx(
                out=ow[:, cols].bitcast(FP8X4), scales=osc[:, cols], in_=woven[:].rearrange("p j t -> p (j t)")
            )
            nc.sync.dma_start(out=out_words[:, cols], in_=ow[:, cols].bitcast(I32))

        leave_a(0, nc.scalar.copy)
        leave_a(1, nc.scalar.copy)
        fetch_far(0)
        turn_near(0)
        turn_near(1)
        turn_far(0)
        fetch_a(0, 0)
        leave_a(2, nc.scalar.copy)
        invert(0)
        leave_a(3, nc.vector.tensor_copy)
        fetch_a(0, 1)
        invert(1)
        fetch_far(1)
        turn_near(2)
        turn_near(3)
        turn_far(1)
        for c in range(len(CHUNKS)):
            if c > 0:
                fetch_a(c, 0)
                fetch_a(c, 1)
            if c in (1, 2):
                invert(c + 1)
            subtract(c, 0)
            subtract(c, 1)
            multiply(c)
            hand_on(c, False)
        for q in range(QUADS):
            queue = nc.sync if q % 2 == 0 else nc.scalar
            queue.dma_start(out=out_2[0, 4 * q : 4 * q + 4, :].bitcast(I32), in_=osc[32 * q : 32 * q + 4, :].bitcast(I32))
